import numpy as np, ml_dtypes
CORES = [6,15,38,47]
N = 4
import mx_ref
BF = ml_dtypes.bfloat16
def entries(a):
    return np.ascontiguousarray(a.T).reshape(-1)
def table(e):
    return np.ascontiguousarray(np.reshape(e, (-1, 16)).T).astype(np.int32)
def gpick(z, e):
    return np.concatenate([z[16 * g:16 * g + 16][:, e[g]] for g in range(8)])
def tile(rs):
    return np.stack(rs, axis=2).reshape(128, -1).astype(BF)
def cut(t, i, w=512):
    return t[:, w * i:w * i + w]
def f(rng, *shape):
    return mx_ref.flush((rng.standard_normal(shape, dtype=np.float32) * np.exp2(rng.integers(-2, 3, shape[:-1] + (1,)))).astype(BF))
def wide(rng, *shape, cols=0):
    v = rng.standard_normal(shape, dtype=np.float32) * np.exp2(rng.integers(-12, 13, shape)).astype(np.float32)
    if cols: v *= np.repeat(np.exp2(rng.integers(-cols, cols + 1, shape[:-2] + (1, shape[-1] // 4))) * (rng.random(shape[:-2] + (1, shape[-1] // 4)) > 0.0625), 4, axis=-1).astype(np.float32)
    return mx_ref.flush(v.astype(BF))
TQ, O = 128, 2
def lay(k, q):
    return {"kp": np.repeat(k, 16, axis=1).astype(np.int32), "qp": np.stack([table(e) for e in q])}
def setup_inputs(rng):
    d = {"qx": f(rng, N, 128, 4 * TQ), "ky": f(rng, N, 128, 2048), "rt": np.repeat(f(rng, 1, 128, 1024), N, axis=0), "vv": f(rng, N, 128, 512 * O)}
    a = rng.integers(0, 3585)
    k = a + rng.integers(0, 512, (N, 8, 4))
    q = np.where(rng.random((N, TQ)) < 0.25, rng.integers(0, 4096, (N, TQ)), a + rng.integers(0, 512, (N, TQ)))
    return {**d, **lay(k, q)}
def setup_inputs_far(rng):
    d = setup_inputs(rng)
    k = rng.integers(1500, 2501, (N, 32)); q = np.zeros((N, TQ), int); a = int(rng.integers(0, 2))
    for r in range(N):
        k[r, rng.permutation(32)[:2]] = [1500, 2500]
        lo, hi = (2628, 4095) if (r + a) % 2 else (0, 1371)
        q[r] = rng.integers(lo, hi + 1, TQ)
        q[r, rng.permutation(TQ)[:2]] = [lo, hi]
    return {**d, **lay(k.reshape(N, 8, 4), q)}
def setup_inputs_same(rng):
    d = setup_inputs(rng); a = int(rng.integers(0, 4096))
    return {**d, **lay(np.full((N, 8, 4), a), np.full((N, TQ), a))}
def setup_inputs_descending(rng):
    d = setup_inputs(rng); a = rng.integers(0, 3585)
    q = np.stack([a + np.sort(rng.permutation(512)[:TQ])[::-1] for r in range(N)])
    k = np.stack([a + 16 * rng.permutation(32) + rng.integers(0, 16, 32) for r in range(N)])
    return {**d, **lay(k.reshape(N, 8, 4), q)}
def setup_inputs_near(rng):
    d = setup_inputs(rng); a = rng.integers(2049, 3968)
    q = np.stack([a + rng.permutation(TQ) % 128 for r in range(N)])
    k = np.stack([a + rng.permutation(np.concatenate([[0, 128], 1 + rng.permutation(127)[:30]])) for r in range(N)])
    return {**d, **lay(k.reshape(N, 8, 4), q)}
def setup_inputs_spread(rng):
    d = setup_inputs(rng); d["qx"] = wide(rng, N, 128, 4 * TQ, cols=4); return d
def check_inputs(d):
    b = []
    for r in range(N):
        k, q = d["kp"][r], entries(d["qp"][r])
        if d["rt"][r].tobytes() != d["rt"][0].tobytes(): b.append("rt")
        if k.min() < 0 or k.max() > 4095 or (k != np.repeat(k[::16], 16, axis=0)).any(): b.append("kp")
        if q.min() < 0 or q.max() > 4095: b.append("qp")
    return b
def reference(qx, ky, rt, vv, kp, qp):
    y = np.zeros((N, 128, O * TQ), np.float32)
    X = [mx_ref.quantize(qx[r]) for r in range(N)]
    for s in range(N):
        K = [mx_ref.quantize(np.ascontiguousarray(cut(ky[s], b))) for b in range(4)]
        V = [mx_ref.quantize(np.ascontiguousarray(cut(vv[s], o))) for o in range(O)]
        R = mx_ref.quantize(rt[s])
        P = [mx_ref.matmul(K[b], R) for b in range(4)]
        for r in range(N):
            A = []
            for b in range(4):
                c = np.clip(entries(qp[r])[None, :] - kp[s][::16, b][:, None], -128, 127) + 128
                A.append(np.maximum(mx_ref.matmul(K[b], X[r]) + gpick(P[b], c), np.float32(0)) * np.float32(0.03125))
            A = mx_ref.quantize(tile(A))
            for o in range(O): y[r][:, TQ * o:TQ * o + TQ] += mx_ref.matmul(V[o], A)
    return {"y": y}

@@ -1,0 +1,326 @@
+from concourse.bass import DstId, RemoteDMATransfer
+from concourse.mybir import dt, AluOpType, ActivationFunctionType
+
+F, B, I32, U16 = "float32", "bfloat16", "int32", "uint16"
+C8, U8 = "float8_e4m3fn_x4", "uint8"
+SCRATCH = {
+    "xb": ("sbuf", [128, 512], B), "kb": ("sbuf", [128, 2048], B), "rb": ("sbuf", [128, 1024], B), "vb": ("sbuf", [128, 1024], B),
+    "kpi": ("sbuf", [128, 4], I32), "kpf": ("sbuf", [128, 4], F), "qpo": ("sbuf", [128, 8], I32),
+    "xq": ("sbuf", [128, 128], C8), "xs": ("sbuf", [128, 128], U8), "kq": ("sbuf", [128, 512], C8), "ks": ("sbuf", [128, 512], U8),
+    "rq": ("sbuf", [128, 256], C8), "rs": ("sbuf", [128, 256], U8), "vq": ("sbuf", [128, 256], C8), "vs": ("sbuf", [128, 256], U8),
+    "qpl": ("sbuf", [128, 24], I32), "xlq": ("sbuf", [128, 384], C8), "xls": ("sbuf", [128, 384], U8),
+    "vlq": ("sbuf", [128, 768], C8), "vls": ("sbuf", [128, 768], U8), "alq": ("sbuf", [128, 384], C8), "als": ("sbuf", [128, 384], U8),
+    "hq": ("sbuf", [128, 128], C8),
+    "dr": ("sbuf", [128, 96], F), "offr": ("sbuf", [128, 96], U16), "do": ("sbuf", [128, 32], F), "offo": ("sbuf", [128, 32], U16),
+    "pw": ("sbuf", [128, 1024], F), "gr": ("sbuf", [128, 1536], F), "go": ("sbuf", [128, 512], F),
+    "u": ("sbuf", [128, 2048], F), "h0": ("sbuf", [128, 512], B), "h1": ("sbuf", [128, 512], B), "h2": ("sbuf", [128, 512], B), "h3": ("sbuf", [128, 512], B),
+    "aq": ("sbuf", [128, 512], C8), "asc": ("sbuf", [128, 512], U8),
+    "yb": ("sbuf", [128, 256], F),
+    "ps": ("psum", [128, 4096], F),
+}
+SEMAPHORES = (["ldx", "ldv", "ldr", "ldk0", "ldk1", "ldkp", "ldqp", "qx", "qv", "qr", "qk0", "qk1", "kpf", "d1", "d1o", "offr", "offo",
+               "qpa", "vh", "hkp", "hk0", "hk1", "sent", "yc", "st"]
+              + [n + str(b) for n in ("p", "pc", "g", "go", "xa", "va", "aa", "rl", "qa") for b in range(4)]
+              + [n + "%d%d" % (k, b) for n in ("s", "ad") for k in range(4) for b in range(4)] + ["y0", "y1"])
+ADD, SUB, MAX, MIN = AluOpType.add, AluOpType.subtract, AluOpType.max, AluOpType.min
+COPY, RELU = ActivationFunctionType.Copy, ActivationFunctionType.Relu
+TWIN = 2
+MINE = [k for k in range(3) if k != TWIN]
+
+
+def bits(engines):
+    return sum(1 << e for e in engines)
+
+
+def peers_of(rank, T, topo):
+    me = topo.chip(T.cores[rank])
+
+    def relation(r):
+        c = topo.chip(T.cores[r])
+        return 1 if topo.mates(me, c) else 2 if topo.same_plane(me, c) else 0
+    return sorted((r for r in range(len(T.cores)) if r != rank), key=relation)
+
+
+def free_writers(rank, T, topo, same_die):
+    me = T.cores[rank]
+    far = [T.cores[r] for r in range(len(T.cores)) if r != rank]
+    return [c for c in topo.cores_of(me)
+            if c != me and (topo.die(c) == topo.die(me)) == same_die and all(topo.may_write(c, d) for d in far)]
+
+
+def relays_of(rank, T, topo):
+    return free_writers(rank, T, topo, False)[:2]
+
+
+def twin_of(rank, T, topo):
+    return free_writers(rank, T, topo, True)[0]
+
+
+def ids(cores, topo):
+    a = [topo.addr(c) for c in cores]
+    return [DstId(rid=x[0], pnc=x[1]) for x in a]
+
+
+def transfer(topo, cores, engines, src, dsts, sem):
+    return RemoteDMATransfer(dst_ids=ids(cores, topo), dma_engine_mask=bits(engines), remote_sem=sem, srcs=[src], dsts=dsts, alu_op=0)
+
+
+def cast(g, topo, me, cores, src, dsts, sem, local_sem):
+    eng = [e for e in topo.engines(me, cores[0]) if all(e in topo.engines(me, c) for c in cores)]
+    g.remote_dma_fused([transfer(topo, cores, eng, src, dsts, sem)], local_sem=local_sem)
+    return len(eng)
+
+
+def u8(v):
+    return v.bitcast(dt.uint8)
+
+
+def cols(i, n=128):
+    return slice(n * i, n * i + n)
+
+
+def relay_program(g, core, T, topo, rank, o):
+    s = T.sem
+    cores = [T.cores[r] for r in peers_of(rank, T, topo)]
+    g.wait_ge(s.vh, 4)
+    n = cast(g, topo, core, cores, u8(T.hq[:, 0:128]), [u8(T.vlq[:, cols(2 * k + o)]) for k in range(3)], s["va%d" % rank], s.sent)
+    g.wait_ge(s.sent, n)
+
+
+def bank(T, i, n):
+    return T.ps[:, 512 * i:512 * i + n]
+
+
+def window(T, b):
+    return T.pw[:, cols(b, 256)]
+
+
+def kside(T, b):
+    return T.kq[:, cols(b)], T.ks[:, cols(b)]
+
+
+def offsets(v, T, q, n, d, off, d1, done):
+    s = T.sem
+    for b in range(4):
+        v.tensor_scalar(d[:, n * b:n * b + n], q, T.kpf[:, b:b + 1], -128.0, SUB, MAX).then_inc(s[d1], 1)
+    v.wait_ge(s[d1], 4)
+    v.tensor_scalar(off[:, 0:4 * n], d[:, 0:4 * n], 127.0, 128.0, MIN, ADD).then_inc(s[done], 1)
+
+
+def ublk(T, k, b):
+    return T.u[:, cols(4 * k + b)]
+
+
+def sums(v, T, k, bs, first, picked, gname):
+    s = T.sem
+    for b in bs:
+        v.wait_ge(s[gname % b], 1)
+        v.wait_ge(s["s%d%d" % (k, b)], 1)
+        v.tensor_tensor(ublk(T, k, b), bank(T, first + b, 128), picked(b), ADD).then_inc(s["ad%d%d" % (k, b)], 1)
+
+
+def relus(a, T, k):
+    s = T.sem
+    for b in range(4):
+        a.wait_ge(s["ad%d%d" % (k, b)], 1)
+        a.activation(T["h%d" % k][:, b:512:4], ublk(T, k, b), RELU, scale=0.03125).then_inc(s["rl%d" % k], 1)
+
+
+def quant_tile(v, T, k):
+    s = T.sem
+    v.wait_ge(s["rl%d" % k], 4)
+    v.quantize_mx(T.aq[:, cols(k)], T.asc[:, cols(k)], T["h%d" % k][:, 0:512]).then_inc(s["qa%d" % k], 1)
+
+
+def send_tile(g, T, topo, me, rank, k, to):
+    s = T.sem
+    g.wait_ge(s["qa%d" % k], 1)
+    n = cast(g, topo, me, [to], u8(T.aq[:, cols(k)]), [u8(T.alq[:, cols(k)])], s["aa%d" % rank], s.sent)
+    return n + cast(g, topo, me, [to], T.asc[:, cols(k)], [T.als[:, cols(k)]], s["aa%d" % rank], s.sent)
+
+
+def twin_program(g, core, T, topo, rank):
+    s, v, a, t = T.sem, g.vector, g.scalar, g.tensor
+    peers = peers_of(rank, T, topo)
+    k, peer = TWIN, peers[TWIN]
+    x = T.xlq[:, cols(k)], T.xls[:, cols(k)]
+    for b in range(4):
+        if b % 2 == 0:
+            t.wait_ge(s["hk%d" % (b // 2)], 16)
+        t.matmul_mx(bank(T, b, 256), *kside(T, b), T.rq[:, 0:256], T.rs[:, 0:256], True, True).then_inc(s["p%d" % b], 1)
+    t.wait_ge(s["xa%d" % peer], 16)
+    for b in range(4):
+        t.matmul_mx(bank(T, 4 + b, 128), *kside(T, b), *x, True, True).then_inc(s["s%d%d" % (k, b)], 1)
+    v.wait_ge(s.hkp, 8)
+    v.tensor_copy(T.kpf[:, 0:4], T.kpi[:, 0:4]).then_inc(s.kpf, 1)
+    v.wait_ge(s.kpf, 1)
+    v.wait_ge(s.qpa, 8)
+    offsets(v, T, T.qpl[:, 8 * k:8 * k + 8], 8, T.do, T.offo, "d1o", "offo")
+    a.wait_ge(s.offo, 1)
+    v.wait_ge(s.offo, 1)
+    for b in range(4):
+        q, copy = (v, v.tensor_copy) if b % 2 else (a, lambda o, i: a.activation(o, i, COPY))
+        q.wait_ge(s["p%d" % b], 1)
+        copy(window(T, b), bank(T, b, 256)).then_inc(s["pc%d" % b], 1)
+        q.wait_ge(s["pc%d" % b], 1)
+        copy(T.go[:, cols(b)], window(T, b).indirect(T.offo[:, cols(b, 8)])).then_inc(s["go%d" % b], 1)
+    sums(v, T, k, range(4), 4, lambda b: T.go[:, cols(b)], "go%d")
+    relus(a, T, k)
+    quant_tile(v, T, k)
+    g.wait_ge(s.vh, 8)
+    n = cast(g, topo, core, [T.cores[r] for r in peers], T.vs[:, 0:256], [T.vls[:, cols(i, 256)] for i in range(3)], s["va%d" % rank], s.sent)
+    n += send_tile(g, T, topo, core, rank, k, T.cores[peer])
+    g.wait_ge(s.sent, n)
+
+
+def rank_program(g, core, T, topo):
+    rank = T.rank_of(core)
+    if rank is None:
+        for r in range(len(T.cores)):
+            hs = relays_of(r, T, topo)
+            if core in hs:
+                relay_program(g, core, T, topo, r, hs.index(core))
+            if core == twin_of(r, T, topo):
+                twin_program(g, core, T, topo, r)
+        return
+    s, v, a, t = T.sem, g.vector, g.scalar, g.tensor
+    peers = peers_of(rank, T, topo)
+    cores = [T.cores[r] for r in peers]
+    hs = relays_of(rank, T, topo)
+    twin = twin_of(rank, T, topo)
+    makers = [twin_of(r, T, topo) if k == TWIN else T.cores[r] for k, r in enumerate(peers)]
+    nm = len(MINE)
+
+    def load_qp(q, i):
+        q.dma_start(T.qpo[16 * i:16 * i + 16, :], T.qp[:, :]).then_inc(s.ldqp, 16)
+    g.sync.dma_start(T.xb[:, :], T.qx[:, :]).then_inc(s.ldx, 16)
+    for i in range(4):
+        load_qp(g.sync, i)
+        load_qp(a, i + 4)
+    a.dma_start(T.kpi[:, :], T.kp[:, :]).then_inc(s.ldkp, 16)
+    g.sync.dma_start(T.rb[:, :], T.rt[:, :]).then_inc(s.ldr, 16)
+    a.dma_start(T.kb[:, 0:1024], T.ky[:, 0:1024]).then_inc(s.ldk0, 16)
+    g.sync.dma_start(T.kb[:, 1024:2048], T.ky[:, 1024:2048]).then_inc(s.ldk1, 16)
+    a.dma_start(T.vb[:, :], T.vv[:, :]).then_inc(s.ldv, 16)
+
+    off = topo.engines(core, cores[0])
+    on = [e for e in topo.engines(core, twin) if e not in off]
+    lo, hi = on[:len(on) // 2], on[len(on) // 2:]
+    sent = 0
+
+    def inside(sem, *transfers):
+        g.remote_dma_fused([transfer(topo, [c], e, src, [dst], sem) for c, e, src, dst in transfers], local_sem=s.sent)
+        return sum(len(x[1]) for x in transfers)
+    g.wait_ge(s.ldqp, 128)
+    sent += cast(g, topo, core, makers, T.qpo[:, 0:8], [T.qpl[:, cols(k, 8)] for k in range(3)], s.qpa, s.sent)
+    g.wait_ge(s.qx, 1)
+    sent += cast(g, topo, core, makers, u8(T.xq[:, 0:128]), [u8(T.xlq[:, cols(k)]) for k in range(3)], s["xa%d" % rank], s.sent)
+    sent += cast(g, topo, core, makers, T.xs[:, 0:128], [T.xls[:, cols(k)] for k in range(3)], s["xa%d" % rank], s.sent)
+    g.wait_ge(s.ldkp, 16)
+    sent += inside(s.hkp, (twin, on, T.kpi[:, 0:4], T.kpi[:, 0:4]))
+    g.wait_ge(s.qr, 1)
+    g.wait_ge(s.qk0, 1)
+    for x, c in ((u8(T.rq[:, 0:256]), u8(T.kq[:, 0:256])), (T.rs[:, 0:256], T.ks[:, 0:256])):
+        sent += inside(s.hk0, (twin, lo, x, x), (twin, hi, c, c))
+    g.wait_ge(s.qk1, 1)
+    for c in (u8(T.kq[:, 256:512]), T.ks[:, 256:512]):
+        sent += inside(s.hk1, (twin, off, c, c))
+    g.wait_ge(s.qv, 1)
+    sent += inside(s.vh, *((hs[o], (lo, hi)[o], u8(T.vq[:, cols(o)]), u8(T.hq[:, 0:128])) for o in range(2)))
+    sent += inside(s.vh, (twin, on, T.vs[:, 0:256], T.vs[:, 0:256]))
+    for k in MINE:
+        sent += send_tile(g, T, topo, core, rank, k, cores[k])
+    g.wait_ge(s.sent, sent)
+
+    t.wait_ge(s.qr, 1)
+    for b in range(4):
+        if b % 2 == 0:
+            t.wait_ge(s["qk%d" % (b // 2)], 1)
+        t.matmul_mx(bank(T, b, 256), *kside(T, b), T.rq[:, 0:256], T.rs[:, 0:256], True, True).then_inc(s["p%d" % b], 1)
+    seq = MINE + [3]
+    first = {k: 4 - 4 * (i % 2) for i, k in enumerate(seq)}
+    for i, k in enumerate(seq):
+        if k == 3:
+            t.wait_ge(s.qx, 1)
+            x = T.xq[:, 0:128], T.xs[:, 0:128]
+        else:
+            t.wait_ge(s["xa%d" % peers[k]], 16)
+            x = T.xlq[:, cols(k)], T.xls[:, cols(k)]
+        for b in range(4):
+            if i == 1:
+                t.wait_ge(s["pc%d" % b], 1)
+            if i > 1:
+                t.wait_ge(s["ad%d%d" % (seq[i - 2], b)], 1)
+            t.matmul_mx(bank(T, first[k] + b, 128), *kside(T, b), *x, True, True).then_inc(s["s%d%d" % (k, b)], 1)
+    yb = first[seq[-2]]
+    for o in range(2):
+        t.wait_ge(s["ad%d%d" % (seq[-2], o)], 1)
+    t.wait_ge(s.qv, 1)
+    t.wait_ge(s.qa3, 1)
+    for o in range(2):
+        t.matmul_mx(bank(T, yb + o, 128), T.vq[:, cols(o)], T.vs[:, cols(o)], T.aq[:, cols(3)], T.asc[:, cols(3)], True, False)
+    for k in range(3):
+        t.wait_ge(s["va%d" % peers[k]], 24)
+        t.wait_ge(s["aa%d" % peers[k]], 16)
+        for o in range(2):
+            w = cols(2 * k + o)
+            m = t.matmul_mx(bank(T, yb + o, 128), T.vlq[:, w], T.vls[:, w], T.alq[:, cols(k)], T.als[:, cols(k)], False, k == 2)
+            if k == 2:
+                m.then_inc(s["y%d" % o], 1)
+
+    def quant(sem, q, sc, x, waited):
+        v.wait_ge(s[waited], 16)
+        v.quantize_mx(q, sc, x).then_inc(s[sem], 1)
+
+    def picked(k):
+        return lambda b: T.gr[:, cols(nm * b + MINE.index(k))] if k < 3 else T.go[:, cols(b)]
+
+    quant("qx", T.xq[:, 0:128], T.xs[:, 0:128], T.xb[:, 0:512], "ldx")
+    quant("qr", T.rq[:, 0:256], T.rs[:, 0:256], T.rb[:, 0:1024], "ldr")
+    quant("qk0", T.kq[:, 0:256], T.ks[:, 0:256], T.kb[:, 0:1024], "ldk0")
+    v.wait_ge(s.ldkp, 16)
+    v.tensor_copy(T.kpf[:, 0:4], T.kpi[:, 0:4]).then_inc(s.kpf, 1)
+    quant("qk1", T.kq[:, 256:512], T.ks[:, 256:512], T.kb[:, 1024:2048], "ldk1")
+    quant("qv", T.vq[:, 0:256], T.vs[:, 0:256], T.vb[:, 0:1024], "ldv")
+    v.wait_ge(s.kpf, 1)
+    v.wait_ge(s.qpa, 8 * nm)
+    offsets(v, T, T.qpl[:, 0:8 * nm], 8 * nm, T.dr, T.offr, "d1", "offr")
+    v.wait_ge(s.offr, 1)
+    for b in (0, 2):
+        v.wait_ge(s["pc%d" % b], 1)
+        v.tensor_copy(T.gr[:, cols(b, 128 * nm)], window(T, b).indirect(T.offr[:, cols(b, 8 * nm)])).then_inc(s["g%d" % b], 1)
+    sums(v, T, MINE[0], range(4), first[MINE[0]], picked(MINE[0]), "g%d")
+    for k, nxt in zip(MINE, MINE[1:]):
+        sums(v, T, nxt, (0,), first[nxt], picked(nxt), "g%d")
+        quant_tile(v, T, k)
+        sums(v, T, nxt, (1, 2, 3), first[nxt], picked(nxt), "g%d")
+    v.wait_ge(s.ldqp, 128)
+    offsets(v, T, T.qpo[:, 0:8], 8, T.do, T.offo, "d1o", "offo")
+    quant_tile(v, T, MINE[-1])
+    v.wait_ge(s.offo, 1)
+    for b in (0, 2):
+        v.tensor_copy(T.go[:, cols(b)], window(T, b).indirect(T.offo[:, cols(b, 8)])).then_inc(s["go%d" % b], 1)
+    sums(v, T, 3, range(4), first[3], picked(3), "go%d")
+    quant_tile(v, T, 3)
+    v.wait_ge(s.y0, 1)
+    v.tensor_copy(T.yb[:, 0:128], bank(T, yb, 128)).then_inc(s.yc, 1)
+
+    for b in range(4):
+        a.wait_ge(s["p%d" % b], 1)
+        a.activation(window(T, b), bank(T, b, 256), COPY).then_inc(s["pc%d" % b], 1)
+    a.wait_ge(s.offr, 1)
+    for b in (1, 3):
+        a.wait_ge(s["pc%d" % b], 1)
+        a.activation(T.gr[:, cols(b, 128 * nm)], window(T, b).indirect(T.offr[:, cols(b, 8 * nm)]), COPY).then_inc(s["g%d" % b], 1)
+    for k in MINE:
+        relus(a, T, k)
+    a.wait_ge(s.offo, 1)
+    for b in (1, 3):
+        a.activation(T.go[:, cols(b)], window(T, b).indirect(T.offo[:, cols(b, 8)]), COPY).then_inc(s["go%d" % b], 1)
+    relus(a, T, 3)
+    a.wait_ge(s.y1, 1)
+    a.activation(T.yb[:, 128:256], bank(T, yb + 1, 128), COPY).then_inc(s.yc, 1)
+
+    g.sync.wait_ge(s.yc, 2)
+    g.sync.dma_start(T.y[:, :], T.yb[:, :]).then_inc(s.st, 16)
+    g.sync.wait_ge(s.st, 16)

@@ -5,27 +5,23 @@ F, B, I32, U16 = "float32", "bfloat16", "int32", "uint16"
 C8, U8 = "float8_e4m3fn_x4", "uint8"
 SCRATCH = {
     "xb": ("sbuf", [128, 512], B), "kb": ("sbuf", [128, 2048], B), "rb": ("sbuf", [128, 1024], B), "vb": ("sbuf", [128, 1024], B),
-    "kpi": ("sbuf", [128, 4], I32), "kpf": ("sbuf", [128, 4], F), "qpo": ("sbuf", [128, 8], I32),
-    "xq": ("sbuf", [128, 128], C8), "xs": ("sbuf", [128, 128], U8), "kq": ("sbuf", [128, 512], C8), "ks": ("sbuf", [128, 512], U8),
-    "rq": ("sbuf", [128, 256], C8), "rs": ("sbuf", [128, 256], U8), "vq": ("sbuf", [128, 256], C8), "vs": ("sbuf", [128, 256], U8),
-    "qpl": ("sbuf", [128, 24], I32), "xlq": ("sbuf", [128, 384], C8), "xls": ("sbuf", [128, 384], U8),
+    "kpi": ("sbuf", [128, 4], I32), "kpf": ("sbuf", [128, 4], F),
+    "kq": ("sbuf", [128, 768], C8), "ks": ("sbuf", [128, 768], U8), "vq": ("sbuf", [128, 256], C8), "vs": ("sbuf", [128, 256], U8),
+    "qi": ("sbuf", [128, 8], I32), "ql": ("sbuf", [128, 32], I32), "xq": ("sbuf", [128, 512], C8), "xs": ("sbuf", [128, 512], U8),
     "vlq": ("sbuf", [128, 768], C8), "vls": ("sbuf", [128, 768], U8), "alq": ("sbuf", [128, 384], C8), "als": ("sbuf", [128, 384], U8),
     "hq": ("sbuf", [128, 128], C8),
-    "dr": ("sbuf", [128, 96], F), "offr": ("sbuf", [128, 96], U16), "do": ("sbuf", [128, 32], F), "offo": ("sbuf", [128, 32], U16),
-    "pw": ("sbuf", [128, 1024], F), "gr": ("sbuf", [128, 1536], F), "go": ("sbuf", [128, 512], F),
-    "u": ("sbuf", [128, 2048], F), "h0": ("sbuf", [128, 512], B), "h1": ("sbuf", [128, 512], B), "h2": ("sbuf", [128, 512], B), "h3": ("sbuf", [128, 512], B),
-    "aq": ("sbuf", [128, 512], C8), "asc": ("sbuf", [128, 512], U8),
+    "off": ("sbuf", [128, 128], U16), "pw": ("sbuf", [128, 1024], F), "gr": ("sbuf", [128, 2048], F),
+    "h": ("sbuf", [128, 2048], B), "aq": ("sbuf", [128, 512], C8), "asc": ("sbuf", [128, 512], U8),
     "yb": ("sbuf", [128, 256], F),
     "ps": ("psum", [128, 4096], F),
 }
-SEMAPHORES = (["ldx", "ldv", "ldr", "ldk0", "ldk1", "ldkp", "ldqp", "qx", "qv", "qr", "qk0", "qk1", "kpf", "d1", "d1o", "offr", "offo",
-               "qpa", "vh", "hkp", "hk0", "hk1", "sent", "yc", "st"]
-              + [n + str(b) for n in ("p", "pc", "g", "go", "xa", "va", "aa", "rl", "qa") for b in range(4)]
-              + [n + "%d%d" % (k, b) for n in ("s", "ad") for k in range(4) for b in range(4)] + ["y0", "y1"])
-ADD, SUB, MAX, MIN = AluOpType.add, AluOpType.subtract, AluOpType.max, AluOpType.min
+SEMAPHORES = (["ldx", "ldv", "ldr", "ldk0", "ldk1", "ldkp", "ldqp", "qx", "qv", "qr", "qk0", "qk1", "kpf",
+               "qpa", "vh", "sent", "yc0", "yc1", "st", "rep", "rep0", "fill", "hkp", "hk0", "hk1", "hk2", "xh"]
+              + [n + str(b) for n in ("p", "pc", "of", "xa", "va", "aa", "rl", "qa") for b in range(4)]
+              + [n + "%d%d" % (k, b) for n in ("ad", "g", "s") for k in range(4) for b in range(4)] + ["y0", "y1"])
+ADD, SUB, MAX, MIN, MULT = AluOpType.add, AluOpType.subtract, AluOpType.max, AluOpType.min, AluOpType.mult
 COPY, RELU = ActivationFunctionType.Copy, ActivationFunctionType.Relu
-TWIN = 2
-MINE = [k for k in range(3) if k != TWIN]
+LATE, TWIN, OWN = 1, 2, 3
 
 
 def bits(engines):
@@ -56,120 +52,142 @@ def twin_of(rank, T, topo):
     return free_writers(rank, T, topo, True)[0]
 
 
-def ids(cores, topo):
-    a = [topo.addr(c) for c in cores]
-    return [DstId(rid=x[0], pnc=x[1]) for x in a]
-
-
-def transfer(topo, cores, engines, src, dsts, sem):
-    return RemoteDMATransfer(dst_ids=ids(cores, topo), dma_engine_mask=bits(engines), remote_sem=sem, srcs=[src], dsts=dsts, alu_op=0)
-
-
-def cast(g, topo, me, cores, src, dsts, sem, local_sem):
-    eng = [e for e in topo.engines(me, cores[0]) if all(e in topo.engines(me, c) for c in cores)]
-    g.remote_dma_fused([transfer(topo, cores, eng, src, dsts, sem)], local_sem=local_sem)
-    return len(eng)
+def send(g, T, topo, *transfers):
+    def ids(cores):
+        return [DstId(rid=topo.addr(c)[0], pnc=topo.addr(c)[1]) for c in cores]
+    g.remote_dma_fused([RemoteDMATransfer(dst_ids=ids(cs), dma_engine_mask=bits(e), remote_sem=T.sem[sem], srcs=[src], dsts=dsts, alu_op=0)
+                        for cs, e, src, dsts, sem in transfers], local_sem=T.sem.sent)
+    return sum(len(x[1]) for x in transfers)
 
 
 def u8(v):
     return v.bitcast(dt.uint8)
 
 
-def cols(i, n=128):
-    return slice(n * i, n * i + n)
+def cols(i, n=128, k=1):
+    return slice(n * i, n * (i + k))
+
+
+def send_tile(g, T, topo, me, rank, k, to):
+    g.wait_ge(T.sem["qa%d" % k], 1)
+    off = topo.engines(me, to)
+    n = send(g, T, topo, ([to], off, u8(T.aq[:, cols(k)]), [u8(T.alq[:, cols(k)])], "aa%d" % rank))
+    return n + send(g, T, topo, ([to], off, T.asc[:, cols(k)], [T.als[:, cols(k)]], "aa%d" % rank))
 
 
 def relay_program(g, core, T, topo, rank, o):
     s = T.sem
-    cores = [T.cores[r] for r in peers_of(rank, T, topo)]
+    peers = peers_of(rank, T, topo)
+    cores = [T.cores[r] for r in peers]
+    off = topo.engines(core, cores[0])
+    g.wait_ge(s.xh, 4)
+    n = send(g, T, topo, ([cores[LATE]], off, u8(T.xq[:, cols(2 * OWN + o, 64)]), [u8(T.xq[:, cols(2 * LATE + o, 64)])], "xa%d" % rank))
     g.wait_ge(s.vh, 4)
-    n = cast(g, topo, core, cores, u8(T.hq[:, 0:128]), [u8(T.vlq[:, cols(2 * k + o)]) for k in range(3)], s["va%d" % rank], s.sent)
+    far = [k for k in range(3) if k != LATE]
+    n += send(g, T, topo, ([cores[k] for k in far], off, u8(T.hq[:, 0:128]), [u8(T.vlq[:, cols(2 * k + o)]) for k in far], "va%d" % rank))
     g.wait_ge(s.sent, n)
 
 
-def bank(T, i, n):
+def bank(T, i, n=128):
     return T.ps[:, 512 * i:512 * i + n]
 
 
-def window(T, b):
-    return T.pw[:, cols(b, 256)]
-
-
 def kside(T, b):
-    return T.kq[:, cols(b)], T.ks[:, cols(b)]
+    return T.kq[:, cols(2 + b)], T.ks[:, cols(2 + b)]
 
 
-def offsets(v, T, q, n, d, off, d1, done):
-    s = T.sem
-    for b in range(4):
-        v.tensor_scalar(d[:, n * b:n * b + n], q, T.kpf[:, b:b + 1], -128.0, SUB, MAX).then_inc(s[d1], 1)
-    v.wait_ge(s[d1], 4)
-    v.tensor_scalar(off[:, 0:4 * n], d[:, 0:4 * n], 127.0, 128.0, MIN, ADD).then_inc(s[done], 1)
+def product_p(g, T, b):
+    g.tensor.matmul_mx(bank(T, b, 256), *kside(T, b), T.kq[:, 0:256], T.ks[:, 0:256], True, True).then_inc(T.sem["p%d" % b], 1)
 
 
-def ublk(T, k, b):
-    return T.u[:, cols(4 * k + b)]
+def product_s(g, T, first, k, b):
+    g.tensor.matmul_mx(bank(T, first[k] + b), *kside(T, b), T.xq[:, cols(k)], T.xs[:, cols(k)], True, True).then_inc(T.sem["s%d%d" % (k, b)], 1)
 
 
-def sums(v, T, k, bs, first, picked, gname):
-    s = T.sem
-    for b in bs:
-        v.wait_ge(s[gname % b], 1)
+def steps(g, T, first, vector, scalar, extra):
+    s, v, a = T.sem, g.vector, g.scalar
+    made = {}
+    for x in vector + scalar:
+        if x[0] in ("pick", "add", "offs"):
+            made.update({(x[0], k, x[1]): x[2] for k in range(x[2], x[2] + x[3])})
+
+    def wait(q, name, n):
+        q.wait_ge(s[name], n)
+
+    def keys(q):
+        v.tensor_scalar(T.kpf[:, 0:4], T.kpi[:, 0:4], 128.0, None, SUB).then_inc(s.kpf, 1)
+        v.wait_ge(s.kpf, 1)
+
+    def repeat(q, k, n):
+        for i in range(1, 4):
+            v.tensor_copy(T.ql[32 * i:32 * i + 32, cols(k, 8, n)], T.ql[0:32, cols(k, 8, n)]).then_inc(s.rep, 1)
+        v.wait_ge(s.rep, 3)
+
+    def copy(q, b):
+        q.wait_ge(s["p%d" % b], 1)
+        dst, src = T.pw[:, cols(b, 256)], bank(T, b, 256)
+        (v.tensor_copy(dst, src) if q is v else a.activation(dst, src, COPY)).then_inc(s["pc%d" % b], 1)
+
+    def offs(q, _, k, n):
+        for b in range(4):
+            v.tensor_scalar(T.off[:, cols(4 * b + k, 8, n)], T.ql[:, cols(k, 8, n)], T.kpf[:, b:b + 1], 255.0, SUB, MIN).then_inc(s["of%d" % k], 1)
+
+    def pick(q, b, k, n):
+        for j in sorted({made["offs", i, 0] for i in range(k, k + n)}):
+            q.wait_ge(s["of%d" % j], 4)
+        q.wait_ge(s["pc%d" % b], 1)
+        src, dst = T.pw[:, cols(b, 256)].indirect(T.off[:, cols(4 * b + k, 8, n)]), T.gr[:, cols(4 * b + k, 128, n)]
+        (v.tensor_copy(dst, src) if q is v else a.activation(dst, src, COPY)).then_inc(s["g%d%d" % (k, b)], 1)
+
+    def add(q, b, k, n):
+        for j in sorted({made["pick", i, b] for i in range(k, k + n)}):
+            v.wait_ge(s["g%d%d" % (j, b)], 1)
         v.wait_ge(s["s%d%d" % (k, b)], 1)
-        v.tensor_tensor(ublk(T, k, b), bank(T, first + b, 128), picked(b), ADD).then_inc(s["ad%d%d" % (k, b)], 1)
+        v.tensor_tensor(T.h[:, 512 * k + b:512 * (k + n):4], bank(T, first[k] + b, 128 * n), T.gr[:, cols(4 * b + k, 128, n)],
+                        ADD).then_inc(s["ad%d%d" % (k, b)], 1)
 
+    def relu(q, k):
+        for b in range(4):
+            q.wait_ge(s["ad%d%d" % (made["add", k, b], b)], 1)
+        h = T.h[:, cols(k, 512)]
+        v.tensor_scalar(h, h, 0.0, 0.03125, MAX, MULT).then_inc(s["rl%d" % k], 1)
 
-def relus(a, T, k):
-    s = T.sem
-    for b in range(4):
-        a.wait_ge(s["ad%d%d" % (k, b)], 1)
-        a.activation(T["h%d" % k][:, b:512:4], ublk(T, k, b), RELU, scale=0.03125).then_inc(s["rl%d" % k], 1)
+    def relub(q, k, b):
+        q.wait_ge(s["ad%d%d" % (made["add", k, b], b)], 1)
+        h = T.h[:, 512 * k + b:512 * (k + 1):4]
+        (v.tensor_scalar(h, h, 0.0, 0.03125, MAX, MULT) if q is v else a.activation(h, h, RELU, scale=0.03125)).then_inc(s["rl%d" % k], 1)
 
+    def quant(q, k):
+        v.wait_ge(s["rl%d" % k], sum(x[0] in ("relu", "relub") and x[1] == k for x in vector + scalar))
+        v.quantize_mx(T.aq[:, cols(k)], T.asc[:, cols(k)], T.h[:, cols(k, 512)]).then_inc(s["qa%d" % k], 1)
 
-def quant_tile(v, T, k):
-    s = T.sem
-    v.wait_ge(s["rl%d" % k], 4)
-    v.quantize_mx(T.aq[:, cols(k)], T.asc[:, cols(k)], T["h%d" % k][:, 0:512]).then_inc(s["qa%d" % k], 1)
-
-
-def send_tile(g, T, topo, me, rank, k, to):
-    s = T.sem
-    g.wait_ge(s["qa%d" % k], 1)
-    n = cast(g, topo, me, [to], u8(T.aq[:, cols(k)]), [u8(T.alq[:, cols(k)])], s["aa%d" % rank], s.sent)
-    return n + cast(g, topo, me, [to], T.asc[:, cols(k)], [T.als[:, cols(k)]], s["aa%d" % rank], s.sent)
+    calls = {"wait": wait, "repeat": repeat, "keys": keys, "copy": copy, "offs": offs, "pick": pick, "add": add, "relu": relu, "relub": relub, "quant": quant, **extra}
+    for q, xs in ((v, vector), (a, scalar)):
+        for x in xs:
+            calls[x[0]](q, *x[1:])
 
 
 def twin_program(g, core, T, topo, rank):
-    s, v, a, t = T.sem, g.vector, g.scalar, g.tensor
+    s, t = T.sem, g.tensor
     peers = peers_of(rank, T, topo)
-    k, peer = TWIN, peers[TWIN]
-    x = T.xlq[:, cols(k)], T.xls[:, cols(k)]
+    cores = [T.cores[r] for r in peers]
+    k, first = TWIN, {TWIN: 4}
+    for b, writes in enumerate((2, 1, 2, 0)):
+        if writes:
+            t.wait_ge(s["hk%d" % b], 8 * writes)
+        product_p(g, T, b)
+    t.wait_ge(s["xa%d" % peers[k]], 16)
     for b in range(4):
-        if b % 2 == 0:
-            t.wait_ge(s["hk%d" % (b // 2)], 16)
-        t.matmul_mx(bank(T, b, 256), *kside(T, b), T.rq[:, 0:256], T.rs[:, 0:256], True, True).then_inc(s["p%d" % b], 1)
-    t.wait_ge(s["xa%d" % peer], 16)
-    for b in range(4):
-        t.matmul_mx(bank(T, 4 + b, 128), *kside(T, b), *x, True, True).then_inc(s["s%d%d" % (k, b)], 1)
-    v.wait_ge(s.hkp, 8)
-    v.tensor_copy(T.kpf[:, 0:4], T.kpi[:, 0:4]).then_inc(s.kpf, 1)
-    v.wait_ge(s.kpf, 1)
-    v.wait_ge(s.qpa, 8)
-    offsets(v, T, T.qpl[:, 8 * k:8 * k + 8], 8, T.do, T.offo, "d1o", "offo")
-    a.wait_ge(s.offo, 1)
-    v.wait_ge(s.offo, 1)
-    for b in range(4):
-        q, copy = (v, v.tensor_copy) if b % 2 else (a, lambda o, i: a.activation(o, i, COPY))
-        q.wait_ge(s["p%d" % b], 1)
-        copy(window(T, b), bank(T, b, 256)).then_inc(s["pc%d" % b], 1)
-        q.wait_ge(s["pc%d" % b], 1)
-        copy(T.go[:, cols(b)], window(T, b).indirect(T.offo[:, cols(b, 8)])).then_inc(s["go%d" % b], 1)
-    sums(v, T, k, range(4), 4, lambda b: T.go[:, cols(b)], "go%d")
-    relus(a, T, k)
-    quant_tile(v, T, k)
+        product_s(g, T, first, k, b)
+    vector = [("wait", "qpa", 8), ("repeat", k, 1), ("wait", "hkp", 8), ("keys",), ("offs", 0, k, 1), ("copy", 1), ("pick", 1, k, 1),
+              ("copy", 3)] + [("add", b, k, 1) for b in range(4)] + [("relub", k, 3), ("quant", k)]
+    scalar = [("copy", 0), ("pick", 0, k, 1), ("copy", 2), ("pick", 2, k, 1), ("pick", 3, k, 1)] + [("relub", k, b) for b in range(3)]
+    steps(g, T, first, vector, scalar, {})
+    g.wait_ge(s.xh, 8)
+    n = send(g, T, topo, ([cores[LATE]], topo.engines(core, cores[0]), T.xs[:, cols(OWN)], [T.xs[:, cols(LATE)]], "xa%d" % rank))
     g.wait_ge(s.vh, 8)
-    n = cast(g, topo, core, [T.cores[r] for r in peers], T.vs[:, 0:256], [T.vls[:, cols(i, 256)] for i in range(3)], s["va%d" % rank], s.sent)
-    n += send_tile(g, T, topo, core, rank, k, T.cores[peer])
+    n += send(g, T, topo, (cores, topo.engines(core, cores[0]), T.vs[:, 0:256], [T.vls[:, cols(i, 256)] for i in range(3)], "va%d" % rank))
+    n += send_tile(g, T, topo, core, rank, k, cores[k])
     g.wait_ge(s.sent, n)
 
 
@@ -188,16 +206,12 @@ def rank_program(g, core, T, topo):
     cores = [T.cores[r] for r in peers]
     hs = relays_of(rank, T, topo)
     twin = twin_of(rank, T, topo)
-    makers = [twin_of(r, T, topo) if k == TWIN else T.cores[r] for k, r in enumerate(peers)]
-    nm = len(MINE)
+    makers = cores[:TWIN] + [twin_of(peers[TWIN], T, topo)]
 
-    def load_qp(q, i):
-        q.dma_start(T.qpo[16 * i:16 * i + 16, :], T.qp[:, :]).then_inc(s.ldqp, 16)
+    for i, q in enumerate((g.sync, a)):
+        q.dma_start(T.qi[16 * i:16 * i + 16, :], T.qp[:, :]).then_inc(s.ldqp, 16)
     g.sync.dma_start(T.xb[:, :], T.qx[:, :]).then_inc(s.ldx, 16)
-    for i in range(4):
-        load_qp(g.sync, i)
-        load_qp(a, i + 4)
-    a.dma_start(T.kpi[:, :], T.kp[:, :]).then_inc(s.ldkp, 16)
+    a.dma_start(T.kpi[:, 0:4], T.kp[:, :]).then_inc(s.ldkp, 16)
     g.sync.dma_start(T.rb[:, :], T.rt[:, :]).then_inc(s.ldr, 16)
     a.dma_start(T.kb[:, 0:1024], T.ky[:, 0:1024]).then_inc(s.ldk0, 16)
     g.sync.dma_start(T.kb[:, 1024:2048], T.ky[:, 1024:2048]).then_inc(s.ldk1, 16)
@@ -206,121 +220,114 @@ def rank_program(g, core, T, topo):
     off = topo.engines(core, cores[0])
     on = [e for e in topo.engines(core, twin) if e not in off]
     lo, hi = on[:len(on) // 2], on[len(on) // 2:]
-    sent = 0
+    xa = "xa%d" % rank
+    xq, xs = u8(T.xq[:, cols(OWN)]), T.xs[:, cols(OWN)]
+    sent = [0]
 
-    def inside(sem, *transfers):
-        g.remote_dma_fused([transfer(topo, [c], e, src, [dst], sem) for c, e, src, dst in transfers], local_sem=s.sent)
-        return sum(len(x[1]) for x in transfers)
-    g.wait_ge(s.ldqp, 128)
-    sent += cast(g, topo, core, makers, T.qpo[:, 0:8], [T.qpl[:, cols(k, 8)] for k in range(3)], s.qpa, s.sent)
+    def call(*transfers):
+        sent[0] += send(g, T, topo, *transfers)
+
+    def to_twin(engines, x, sem):
+        call(([twin], engines, x, [x], sem))
+    g.wait_ge(s.fill, 2)
+    g.wait_ge(s.ldqp, 32)
+    call((makers, off, T.qi[:, :], [T.ql[:, cols(k, 8)] for k in range(3)], "qpa"))
     g.wait_ge(s.qx, 1)
-    sent += cast(g, topo, core, makers, u8(T.xq[:, 0:128]), [u8(T.xlq[:, cols(k)]) for k in range(3)], s["xa%d" % rank], s.sent)
-    sent += cast(g, topo, core, makers, T.xs[:, 0:128], [T.xls[:, cols(k)] for k in range(3)], s["xa%d" % rank], s.sent)
-    g.wait_ge(s.ldkp, 16)
-    sent += inside(s.hkp, (twin, on, T.kpi[:, 0:4], T.kpi[:, 0:4]))
+    call(*(([hs[o]], (lo, hi)[o], u8(T.xq[:, cols(2 * OWN + o, 64)]), [u8(T.xq[:, cols(2 * OWN + o, 64)])], "xh") for o in range(2)))
+    direct = [k for k in range(3) if k != LATE]
+    call(([makers[k] for k in direct], off, xq, [u8(T.xq[:, cols(k)]) for k in direct], xa))
+    call(([makers[k] for k in direct], off, xs, [T.xs[:, cols(k)] for k in direct], xa), ([twin], on, xs, [xs], "xh"))
     g.wait_ge(s.qr, 1)
     g.wait_ge(s.qk0, 1)
-    for x, c in ((u8(T.rq[:, 0:256]), u8(T.kq[:, 0:256])), (T.rs[:, 0:256], T.ks[:, 0:256])):
-        sent += inside(s.hk0, (twin, lo, x, x), (twin, hi, c, c))
+    to_twin(on, T.ks[:, 0:512], "hk0")
+    to_twin(on, u8(T.kq[:, 0:384]), "hk0")
     g.wait_ge(s.qk1, 1)
-    for c in (u8(T.kq[:, 256:512]), T.ks[:, 256:512]):
-        sent += inside(s.hk1, (twin, off, c, c))
+    to_twin(off, u8(T.kq[:, 512:768]), "hk2")
+    g.wait_ge(s.ldkp, 16)
+    to_twin(on, T.kpi[:, :], "hkp")
+    to_twin(on, u8(T.kq[:, 384:512]), "hk1")
     g.wait_ge(s.qv, 1)
-    sent += inside(s.vh, *((hs[o], (lo, hi)[o], u8(T.vq[:, cols(o)]), u8(T.hq[:, 0:128])) for o in range(2)))
-    sent += inside(s.vh, (twin, on, T.vs[:, 0:256], T.vs[:, 0:256]))
-    for k in MINE:
-        sent += send_tile(g, T, topo, core, rank, k, cores[k])
-    g.wait_ge(s.sent, sent)
+    call(([twin], off, T.ks[:, 512:768], [T.ks[:, 512:768]], "hk2"), ([twin], on, T.vs[:, 0:256], [T.vs[:, 0:256]], "vh"))
+    call(*(([hs[o]], (lo, hi)[o], u8(T.vq[:, cols(o)]), [u8(T.hq[:, 0:128])], "vh") for o in range(2)))
+    call(([cores[LATE]], off, u8(T.vq[:, 0:256]), [u8(T.vlq[:, cols(LATE, 256)])], "va%d" % rank))
+    for k in range(TWIN):
+        sent[0] += send_tile(g, T, topo, core, rank, k, cores[k])
+    g.wait_ge(s.sent, sent[0])
 
     t.wait_ge(s.qr, 1)
     for b in range(4):
         if b % 2 == 0:
             t.wait_ge(s["qk%d" % (b // 2)], 1)
-        t.matmul_mx(bank(T, b, 256), *kside(T, b), T.rq[:, 0:256], T.rs[:, 0:256], True, True).then_inc(s["p%d" % b], 1)
-    seq = MINE + [3]
+        product_p(g, T, b)
+    seq = [0, 1, OWN]
     first = {k: 4 - 4 * (i % 2) for i, k in enumerate(seq)}
     for i, k in enumerate(seq):
-        if k == 3:
+        if k == OWN:
             t.wait_ge(s.qx, 1)
-            x = T.xq[:, 0:128], T.xs[:, 0:128]
         else:
-            t.wait_ge(s["xa%d" % peers[k]], 16)
-            x = T.xlq[:, cols(k)], T.xls[:, cols(k)]
+            t.wait_ge(s["xa%d" % peers[k]], 24 if k == LATE else 16)
         for b in range(4):
             if i == 1:
                 t.wait_ge(s["pc%d" % b], 1)
             if i > 1:
                 t.wait_ge(s["ad%d%d" % (seq[i - 2], b)], 1)
-            t.matmul_mx(bank(T, first[k] + b, 128), *kside(T, b), *x, True, True).then_inc(s["s%d%d" % (k, b)], 1)
+            product_s(g, T, first, k, b)
     yb = first[seq[-2]]
     for o in range(2):
         t.wait_ge(s["ad%d%d" % (seq[-2], o)], 1)
-    t.wait_ge(s.qv, 1)
-    t.wait_ge(s.qa3, 1)
-    for o in range(2):
-        t.matmul_mx(bank(T, yb + o, 128), T.vq[:, cols(o)], T.vs[:, cols(o)], T.aq[:, cols(3)], T.asc[:, cols(3)], True, False)
-    for k in range(3):
-        t.wait_ge(s["va%d" % peers[k]], 24)
-        t.wait_ge(s["aa%d" % peers[k]], 16)
+    order = [0, OWN, 1, 2]
+    for k in order:
+        if k == OWN:
+            t.wait_ge(s.qv, 1)
+            t.wait_ge(s.qa3, 1)
+        else:
+            t.wait_ge(s["va%d" % peers[k]], 16 if k == LATE else 24)
+            t.wait_ge(s["aa%d" % peers[k]], 16)
         for o in range(2):
             w = cols(2 * k + o)
-            m = t.matmul_mx(bank(T, yb + o, 128), T.vlq[:, w], T.vls[:, w], T.alq[:, cols(k)], T.als[:, cols(k)], False, k == 2)
-            if k == 2:
+            sides = (T.vq[:, cols(o)], T.vs[:, cols(o)], T.aq[:, cols(k)], T.asc[:, cols(k)]) if k == OWN else (
+                T.vlq[:, w], T.vls[:, w], T.alq[:, cols(k)], T.als[:, cols(k)])
+            m = t.matmul_mx(bank(T, yb + o), *sides, k == order[0], k == order[-1])
+            if k == order[-1]:
                 m.then_inc(s["y%d" % o], 1)
 
-    def quant(sem, q, sc, x, waited):
-        v.wait_ge(s[waited], 16)
-        v.quantize_mx(q, sc, x).then_inc(s[sem], 1)
+    inputs = {"qx": (T.xq[:, cols(OWN)], T.xs[:, cols(OWN)], T.xb[:, 0:512], "ldx"),
+              "qr": (T.kq[:, 0:256], T.ks[:, 0:256], T.rb[:, 0:1024], "ldr"),
+              "qk0": (T.kq[:, 256:512], T.ks[:, 256:512], T.kb[:, 0:1024], "ldk0"),
+              "qk1": (T.kq[:, 512:768], T.ks[:, 512:768], T.kb[:, 1024:2048], "ldk1"),
+              "qv": (T.vq[:, 0:256], T.vs[:, 0:256], T.vb[:, 0:1024], "ldv")}
 
-    def picked(k):
-        return lambda b: T.gr[:, cols(nm * b + MINE.index(k))] if k < 3 else T.go[:, cols(b)]
+    def pack(q, name):
+        codes, scales, x, loaded = inputs[name]
+        v.wait_ge(s[loaded], 16)
+        v.quantize_mx(codes, scales, x).then_inc(s[name], 1)
 
-    quant("qx", T.xq[:, 0:128], T.xs[:, 0:128], T.xb[:, 0:512], "ldx")
-    quant("qr", T.rq[:, 0:256], T.rs[:, 0:256], T.rb[:, 0:1024], "ldr")
-    quant("qk0", T.kq[:, 0:256], T.ks[:, 0:256], T.kb[:, 0:1024], "ldk0")
-    v.wait_ge(s.ldkp, 16)
-    v.tensor_copy(T.kpf[:, 0:4], T.kpi[:, 0:4]).then_inc(s.kpf, 1)
-    quant("qk1", T.kq[:, 256:512], T.ks[:, 256:512], T.kb[:, 1024:2048], "ldk1")
-    quant("qv", T.vq[:, 0:256], T.vs[:, 0:256], T.vb[:, 0:1024], "ldv")
-    v.wait_ge(s.kpf, 1)
-    v.wait_ge(s.qpa, 8 * nm)
-    offsets(v, T, T.qpl[:, 0:8 * nm], 8 * nm, T.dr, T.offr, "d1", "offr")
-    v.wait_ge(s.offr, 1)
-    for b in (0, 2):
-        v.wait_ge(s["pc%d" % b], 1)
-        v.tensor_copy(T.gr[:, cols(b, 128 * nm)], window(T, b).indirect(T.offr[:, cols(b, 8 * nm)])).then_inc(s["g%d" % b], 1)
-    sums(v, T, MINE[0], range(4), first[MINE[0]], picked(MINE[0]), "g%d")
-    for k, nxt in zip(MINE, MINE[1:]):
-        sums(v, T, nxt, (0,), first[nxt], picked(nxt), "g%d")
-        quant_tile(v, T, k)
-        sums(v, T, nxt, (1, 2, 3), first[nxt], picked(nxt), "g%d")
-    v.wait_ge(s.ldqp, 128)
-    offsets(v, T, T.qpo[:, 0:8], 8, T.do, T.offo, "d1o", "offo")
-    quant_tile(v, T, MINE[-1])
-    v.wait_ge(s.offo, 1)
-    for b in (0, 2):
-        v.tensor_copy(T.go[:, cols(b)], window(T, b).indirect(T.offo[:, cols(b, 8)])).then_inc(s["go%d" % b], 1)
-    sums(v, T, 3, range(4), first[3], picked(3), "go%d")
-    quant_tile(v, T, 3)
-    v.wait_ge(s.y0, 1)
-    v.tensor_copy(T.yb[:, 0:128], bank(T, yb, 128)).then_inc(s.yc, 1)
+    def fill(q):
+        v.memset(T.qi[32:64, :], 0).then_inc(s.fill, 1)
+        v.memset(T.qi[64:128, :], 0).then_inc(s.fill, 1)
 
-    for b in range(4):
-        a.wait_ge(s["p%d" % b], 1)
-        a.activation(window(T, b), bank(T, b, 256), COPY).then_inc(s["pc%d" % b], 1)
-    a.wait_ge(s.offr, 1)
-    for b in (1, 3):
-        a.wait_ge(s["pc%d" % b], 1)
-        a.activation(T.gr[:, cols(b, 128 * nm)], window(T, b).indirect(T.offr[:, cols(b, 8 * nm)]), COPY).then_inc(s["g%d" % b], 1)
-    for k in MINE:
-        relus(a, T, k)
-    a.wait_ge(s.offo, 1)
-    for b in (1, 3):
-        a.activation(T.go[:, cols(b)], window(T, b).indirect(T.offo[:, cols(b, 8)]), COPY).then_inc(s["go%d" % b], 1)
-    relus(a, T, 3)
-    a.wait_ge(s.y1, 1)
-    a.activation(T.yb[:, 128:256], bank(T, yb + 1, 128), COPY).then_inc(s.yc, 1)
+    def mine(q):
+        v.wait_ge(s.ldqp, 32)
+        for i in range(4):
+            v.tensor_copy(T.ql[32 * i:32 * i + 32, cols(OWN, 8)], T.qi[0:32, :]).then_inc(s.rep0, 1)
+        v.wait_ge(s.rep0, 4)
 
-    g.sync.wait_ge(s.yc, 2)
-    g.sync.dma_start(T.y[:, :], T.yb[:, :]).then_inc(s.st, 16)
-    g.sync.wait_ge(s.st, 16)
+    def out(q, o):
+        q.wait_ge(s["y%d" % o], 1)
+        dst, src = T.yb[:, cols(o)], bank(T, yb + o)
+        (v.tensor_copy(dst, src) if q is v else a.activation(dst, src, COPY)).then_inc(s["yc%d" % o], 1)
+
+    def adds(k, bs=range(4)):
+        return [("add", b, k, 1) for b in bs]
+    vector = [("fill",), ("pack", "qx"), ("mine",), ("wait", "ldkp", 16), ("keys",), ("offs", 0, OWN, 1), ("pack", "qr"), ("pack", "qk0"),
+              ("pack", "qk1"), ("pack", "qv"), ("wait", "qpa", 16), ("repeat", 0, 2), ("offs", 0, 0, 2), ("pick", 0, 0, 1), ("pick", 2, 0, 1)]
+    vector += adds(0) + [("relu", 0), ("quant", 0)] + adds(1) + [("quant", 1)]
+    vector += adds(OWN) + [("relu", OWN), ("quant", OWN), ("out", 0)]
+    scalar = [("copy", b) for b in range(4)] + [("pick", 1, 0, 1), ("pick", 3, 0, 1)] + [("pick", b, 1, 1) for b in range(4)]
+    scalar += [("pick", 0, OWN, 1)] + [("relub", 1, b) for b in range(4)] + [("pick", b, OWN, 1) for b in range(1, 4)] + [("out", 1)]
+    steps(g, T, first, vector, scalar, {"pack": pack, "fill": fill, "mine": mine, "out": out})
+
+    for o, q in enumerate((g.sync, a)):
+        q.wait_ge(s["yc%d" % o], 1)
+        q.dma_start(T.y[:, cols(o)], T.yb[:, cols(o)]).then_inc(s.st, 16)
+    g.sync.wait_ge(s.st, 32)

from concourse.bass import DstId, RemoteDMATransfer
from concourse.mybir import dt, AluOpType, ActivationFunctionType

F, B, I32, U16 = "float32", "bfloat16", "int32", "uint16"
C8, U8 = "float8_e4m3fn_x4", "uint8"
SCRATCH = {
    "xb": ("sbuf", [128, 512], B), "kb": ("sbuf", [128, 2048], B), "rb": ("sbuf", [128, 1024], B), "vb": ("sbuf", [128, 1024], B),
    "kpi": ("sbuf", [128, 4], I32), "kpf": ("sbuf", [128, 4], F),
    "kq": ("sbuf", [128, 768], C8), "ks": ("sbuf", [128, 768], U8), "vq": ("sbuf", [128, 256], C8), "vs": ("sbuf", [128, 256], U8),
    "qi": ("sbuf", [128, 8], I32), "ql": ("sbuf", [128, 32], I32), "xq": ("sbuf", [128, 512], C8), "xs": ("sbuf", [128, 512], U8),
    "vlq": ("sbuf", [128, 768], C8), "vls": ("sbuf", [128, 768], U8), "alq": ("sbuf", [128, 384], C8), "als": ("sbuf", [128, 384], U8),
    "hq": ("sbuf", [128, 128], C8),
    "off": ("sbuf", [128, 128], U16), "pw": ("sbuf", [128, 1024], F), "gr": ("sbuf", [128, 2048], F),
    "h": ("sbuf", [128, 2048], B), "aq": ("sbuf", [128, 512], C8), "asc": ("sbuf", [128, 512], U8),
    "yb": ("sbuf", [128, 256], F),
    "ps": ("psum", [128, 4096], F),
}
SEMAPHORES = (["ldx", "ldv", "ldr", "ldk0", "ldk1", "ldkp", "ldqp", "qx", "qv", "qr", "qk0", "qk1", "kpf",
               "qpa", "vh", "sent", "yc0", "yc1", "st", "rep", "rep0", "fill", "hkp", "hk0", "hk1", "hk2", "xh"]
              + [n + str(b) for n in ("p", "pc", "of", "xa", "va", "aa", "rl", "qa") for b in range(4)]
              + [n + "%d%d" % (k, b) for n in ("ad", "g", "s") for k in range(4) for b in range(4)] + ["y0", "y1"])
ADD, SUB, MAX, MIN, MULT = AluOpType.add, AluOpType.subtract, AluOpType.max, AluOpType.min, AluOpType.mult
COPY, RELU = ActivationFunctionType.Copy, ActivationFunctionType.Relu
LATE, TWIN, OWN = 1, 2, 3


def bits(engines):
    return sum(1 << e for e in engines)


def peers_of(rank, T, topo):
    me = topo.chip(T.cores[rank])

    def relation(r):
        c = topo.chip(T.cores[r])
        return 1 if topo.mates(me, c) else 2 if topo.same_plane(me, c) else 0
    return sorted((r for r in range(len(T.cores)) if r != rank), key=relation)


def free_writers(rank, T, topo, same_die):
    me = T.cores[rank]
    far = [T.cores[r] for r in range(len(T.cores)) if r != rank]
    return [c for c in topo.cores_of(me)
            if c != me and (topo.die(c) == topo.die(me)) == same_die and all(topo.may_write(c, d) for d in far)]


def relays_of(rank, T, topo):
    return free_writers(rank, T, topo, False)[:2]


def twin_of(rank, T, topo):
    return free_writers(rank, T, topo, True)[0]


def send(g, T, topo, *transfers):
    def ids(cores):
        return [DstId(rid=topo.addr(c)[0], pnc=topo.addr(c)[1]) for c in cores]
    g.remote_dma_fused([RemoteDMATransfer(dst_ids=ids(cs), dma_engine_mask=bits(e), remote_sem=T.sem[sem], srcs=[src], dsts=dsts, alu_op=0)
                        for cs, e, src, dsts, sem in transfers], local_sem=T.sem.sent)
    return sum(len(x[1]) for x in transfers)


def u8(v):
    return v.bitcast(dt.uint8)


def cols(i, n=128, k=1):
    return slice(n * i, n * (i + k))


def send_tile(g, T, topo, me, rank, k, to):
    g.wait_ge(T.sem["qa%d" % k], 1)
    off = topo.engines(me, to)
    n = send(g, T, topo, ([to], off, u8(T.aq[:, cols(k)]), [u8(T.alq[:, cols(k)])], "aa%d" % rank))
    return n + send(g, T, topo, ([to], off, T.asc[:, cols(k)], [T.als[:, cols(k)]], "aa%d" % rank))


def relay_program(g, core, T, topo, rank, o):
    s = T.sem
    peers = peers_of(rank, T, topo)
    cores = [T.cores[r] for r in peers]
    off = topo.engines(core, cores[0])
    g.wait_ge(s.xh, 4)
    n = send(g, T, topo, ([cores[LATE]], off, u8(T.xq[:, cols(2 * OWN + o, 64)]), [u8(T.xq[:, cols(2 * LATE + o, 64)])], "xa%d" % rank))
    g.wait_ge(s.vh, 4)
    far = [k for k in range(3) if k != LATE]
    n += send(g, T, topo, ([cores[k] for k in far], off, u8(T.hq[:, 0:128]), [u8(T.vlq[:, cols(2 * k + o)]) for k in far], "va%d" % rank))
    g.wait_ge(s.sent, n)


def bank(T, i, n=128):
    return T.ps[:, 512 * i:512 * i + n]


def kside(T, b):
    return T.kq[:, cols(2 + b)], T.ks[:, cols(2 + b)]


def product_p(g, T, b):
    g.tensor.matmul_mx(bank(T, b, 256), *kside(T, b), T.kq[:, 0:256], T.ks[:, 0:256], True, True).then_inc(T.sem["p%d" % b], 1)


def product_s(g, T, first, k, b):
    g.tensor.matmul_mx(bank(T, first[k] + b), *kside(T, b), T.xq[:, cols(k)], T.xs[:, cols(k)], True, True).then_inc(T.sem["s%d%d" % (k, b)], 1)


def steps(g, T, first, vector, scalar, extra):
    s, v, a = T.sem, g.vector, g.scalar
    made = {}
    for x in vector + scalar:
        if x[0] in ("pick", "add", "offs"):
            made.update({(x[0], k, x[1]): x[2] for k in range(x[2], x[2] + x[3])})

    def wait(q, name, n):
        q.wait_ge(s[name], n)

    def keys(q):
        v.tensor_scalar(T.kpf[:, 0:4], T.kpi[:, 0:4], 128.0, None, SUB).then_inc(s.kpf, 1)
        v.wait_ge(s.kpf, 1)

    def repeat(q, k, n):
        for i in range(1, 4):
            v.tensor_copy(T.ql[32 * i:32 * i + 32, cols(k, 8, n)], T.ql[0:32, cols(k, 8, n)]).then_inc(s.rep, 1)
        v.wait_ge(s.rep, 3)

    def copy(q, b):
        q.wait_ge(s["p%d" % b], 1)
        dst, src = T.pw[:, cols(b, 256)], bank(T, b, 256)
        (v.tensor_copy(dst, src) if q is v else a.activation(dst, src, COPY)).then_inc(s["pc%d" % b], 1)

    def offs(q, _, k, n):
        for b in range(4):
            v.tensor_scalar(T.off[:, cols(4 * b + k, 8, n)], T.ql[:, cols(k, 8, n)], T.kpf[:, b:b + 1], 255.0, SUB, MIN).then_inc(s["of%d" % k], 1)

    def pick(q, b, k, n):
        for j in sorted({made["offs", i, 0] for i in range(k, k + n)}):
            q.wait_ge(s["of%d" % j], 4)
        q.wait_ge(s["pc%d" % b], 1)
        src, dst = T.pw[:, cols(b, 256)].indirect(T.off[:, cols(4 * b + k, 8, n)]), T.gr[:, cols(4 * b + k, 128, n)]
        (v.tensor_copy(dst, src) if q is v else a.activation(dst, src, COPY)).then_inc(s["g%d%d" % (k, b)], 1)

    def add(q, b, k, n):
        for j in sorted({made["pick", i, b] for i in range(k, k + n)}):
            v.wait_ge(s["g%d%d" % (j, b)], 1)
        v.wait_ge(s["s%d%d" % (k, b)], 1)
        v.tensor_tensor(T.h[:, 512 * k + b:512 * (k + n):4], bank(T, first[k] + b, 128 * n), T.gr[:, cols(4 * b + k, 128, n)],
                        ADD).then_inc(s["ad%d%d" % (k, b)], 1)

    def relu(q, k):
        for b in range(4):
            q.wait_ge(s["ad%d%d" % (made["add", k, b], b)], 1)
        h = T.h[:, cols(k, 512)]
        v.tensor_scalar(h, h, 0.0, 0.03125, MAX, MULT).then_inc(s["rl%d" % k], 1)

    def relub(q, k, b):
        q.wait_ge(s["ad%d%d" % (made["add", k, b], b)], 1)
        h = T.h[:, 512 * k + b:512 * (k + 1):4]
        (v.tensor_scalar(h, h, 0.0, 0.03125, MAX, MULT) if q is v else a.activation(h, h, RELU, scale=0.03125)).then_inc(s["rl%d" % k], 1)

    def quant(q, k):
        v.wait_ge(s["rl%d" % k], sum(x[0] in ("relu", "relub") and x[1] == k for x in vector + scalar))
        v.quantize_mx(T.aq[:, cols(k)], T.asc[:, cols(k)], T.h[:, cols(k, 512)]).then_inc(s["qa%d" % k], 1)

    calls = {"wait": wait, "repeat": repeat, "keys": keys, "copy": copy, "offs": offs, "pick": pick, "add": add, "relu": relu, "relub": relub, "quant": quant, **extra}
    for q, xs in ((v, vector), (a, scalar)):
        for x in xs:
            calls[x[0]](q, *x[1:])


def twin_program(g, core, T, topo, rank):
    s, t = T.sem, g.tensor
    peers = peers_of(rank, T, topo)
    cores = [T.cores[r] for r in peers]
    k, first = TWIN, {TWIN: 4}
    for b, writes in enumerate((2, 1, 2, 0)):
        if writes:
            t.wait_ge(s["hk%d" % b], 8 * writes)
        product_p(g, T, b)
    t.wait_ge(s["xa%d" % peers[k]], 16)
    for b in range(4):
        product_s(g, T, first, k, b)
    vector = [("wait", "qpa", 8), ("repeat", k, 1), ("wait", "hkp", 8), ("keys",), ("offs", 0, k, 1), ("copy", 1), ("pick", 1, k, 1),
              ("copy", 3)] + [("add", b, k, 1) for b in range(4)] + [("relub", k, 3), ("quant", k)]
    scalar = [("copy", 0), ("pick", 0, k, 1), ("copy", 2), ("pick", 2, k, 1), ("pick", 3, k, 1)] + [("relub", k, b) for b in range(3)]
    steps(g, T, first, vector, scalar, {})
    g.wait_ge(s.xh, 8)
    n = send(g, T, topo, ([cores[LATE]], topo.engines(core, cores[0]), T.xs[:, cols(OWN)], [T.xs[:, cols(LATE)]], "xa%d" % rank))
    g.wait_ge(s.vh, 8)
    n += send(g, T, topo, (cores, topo.engines(core, cores[0]), T.vs[:, 0:256], [T.vls[:, cols(i, 256)] for i in range(3)], "va%d" % rank))
    n += send_tile(g, T, topo, core, rank, k, cores[k])
    g.wait_ge(s.sent, n)


def rank_program(g, core, T, topo):
    rank = T.rank_of(core)
    if rank is None:
        for r in range(len(T.cores)):
            hs = relays_of(r, T, topo)
            if core in hs:
                relay_program(g, core, T, topo, r, hs.index(core))
            if core == twin_of(r, T, topo):
                twin_program(g, core, T, topo, r)
        return
    s, v, a, t = T.sem, g.vector, g.scalar, g.tensor
    peers = peers_of(rank, T, topo)
    cores = [T.cores[r] for r in peers]
    hs = relays_of(rank, T, topo)
    twin = twin_of(rank, T, topo)
    makers = cores[:TWIN] + [twin_of(peers[TWIN], T, topo)]

    for i, q in enumerate((g.sync, a)):
        q.dma_start(T.qi[16 * i:16 * i + 16, :], T.qp[:, :]).then_inc(s.ldqp, 16)
    g.sync.dma_start(T.xb[:, :], T.qx[:, :]).then_inc(s.ldx, 16)
    a.dma_start(T.kpi[:, 0:4], T.kp[:, :]).then_inc(s.ldkp, 16)
    g.sync.dma_start(T.rb[:, :], T.rt[:, :]).then_inc(s.ldr, 16)
    a.dma_start(T.kb[:, 0:1024], T.ky[:, 0:1024]).then_inc(s.ldk0, 16)
    g.sync.dma_start(T.kb[:, 1024:2048], T.ky[:, 1024:2048]).then_inc(s.ldk1, 16)
    a.dma_start(T.vb[:, :], T.vv[:, :]).then_inc(s.ldv, 16)

    off = topo.engines(core, cores[0])
    on = [e for e in topo.engines(core, twin) if e not in off]
    lo, hi = on[:len(on) // 2], on[len(on) // 2:]
    xa = "xa%d" % rank
    xq, xs = u8(T.xq[:, cols(OWN)]), T.xs[:, cols(OWN)]
    sent = [0]

    def call(*transfers):
        sent[0] += send(g, T, topo, *transfers)

    def to_twin(engines, x, sem):
        call(([twin], engines, x, [x], sem))
    g.wait_ge(s.fill, 2)
    g.wait_ge(s.ldqp, 32)
    call((makers, off, T.qi[:, :], [T.ql[:, cols(k, 8)] for k in range(3)], "qpa"))
    g.wait_ge(s.qx, 1)
    call(*(([hs[o]], (lo, hi)[o], u8(T.xq[:, cols(2 * OWN + o, 64)]), [u8(T.xq[:, cols(2 * OWN + o, 64)])], "xh") for o in range(2)))
    direct = [k for k in range(3) if k != LATE]
    call(([makers[k] for k in direct], off, xq, [u8(T.xq[:, cols(k)]) for k in direct], xa))
    call(([makers[k] for k in direct], off, xs, [T.xs[:, cols(k)] for k in direct], xa), ([twin], on, xs, [xs], "xh"))
    g.wait_ge(s.qr, 1)
    g.wait_ge(s.qk0, 1)
    to_twin(on, T.ks[:, 0:512], "hk0")
    to_twin(on, u8(T.kq[:, 0:384]), "hk0")
    g.wait_ge(s.qk1, 1)
    to_twin(off, u8(T.kq[:, 512:768]), "hk2")
    g.wait_ge(s.ldkp, 16)
    to_twin(on, T.kpi[:, :], "hkp")
    to_twin(on, u8(T.kq[:, 384:512]), "hk1")
    g.wait_ge(s.qv, 1)
    call(([twin], off, T.ks[:, 512:768], [T.ks[:, 512:768]], "hk2"), ([twin], on, T.vs[:, 0:256], [T.vs[:, 0:256]], "vh"))
    call(*(([hs[o]], (lo, hi)[o], u8(T.vq[:, cols(o)]), [u8(T.hq[:, 0:128])], "vh") for o in range(2)))
    call(([cores[LATE]], off, u8(T.vq[:, 0:256]), [u8(T.vlq[:, cols(LATE, 256)])], "va%d" % rank))
    for k in range(TWIN):
        sent[0] += send_tile(g, T, topo, core, rank, k, cores[k])
    g.wait_ge(s.sent, sent[0])

    t.wait_ge(s.qr, 1)
    for b in range(4):
        if b % 2 == 0:
            t.wait_ge(s["qk%d" % (b // 2)], 1)
        product_p(g, T, b)
    seq = [0, 1, OWN]
    first = {k: 4 - 4 * (i % 2) for i, k in enumerate(seq)}
    for i, k in enumerate(seq):
        if k == OWN:
            t.wait_ge(s.qx, 1)
        else:
            t.wait_ge(s["xa%d" % peers[k]], 24 if k == LATE else 16)
        for b in range(4):
            if i == 1:
                t.wait_ge(s["pc%d" % b], 1)
            if i > 1:
                t.wait_ge(s["ad%d%d" % (seq[i - 2], b)], 1)
            product_s(g, T, first, k, b)
    yb = first[seq[-2]]
    for o in range(2):
        t.wait_ge(s["ad%d%d" % (seq[-2], o)], 1)
    order = [0, OWN, 1, 2]
    for k in order:
        if k == OWN:
            t.wait_ge(s.qv, 1)
            t.wait_ge(s.qa3, 1)
        else:
            t.wait_ge(s["va%d" % peers[k]], 16 if k == LATE else 24)
            t.wait_ge(s["aa%d" % peers[k]], 16)
        for o in range(2):
            w = cols(2 * k + o)
            sides = (T.vq[:, cols(o)], T.vs[:, cols(o)], T.aq[:, cols(k)], T.asc[:, cols(k)]) if k == OWN else (
                T.vlq[:, w], T.vls[:, w], T.alq[:, cols(k)], T.als[:, cols(k)])
            m = t.matmul_mx(bank(T, yb + o), *sides, k == order[0], k == order[-1])
            if k == order[-1]:
                m.then_inc(s["y%d" % o], 1)

    inputs = {"qx": (T.xq[:, cols(OWN)], T.xs[:, cols(OWN)], T.xb[:, 0:512], "ldx"),
              "qr": (T.kq[:, 0:256], T.ks[:, 0:256], T.rb[:, 0:1024], "ldr"),
              "qk0": (T.kq[:, 256:512], T.ks[:, 256:512], T.kb[:, 0:1024], "ldk0"),
              "qk1": (T.kq[:, 512:768], T.ks[:, 512:768], T.kb[:, 1024:2048], "ldk1"),
              "qv": (T.vq[:, 0:256], T.vs[:, 0:256], T.vb[:, 0:1024], "ldv")}

    def pack(q, name):
        codes, scales, x, loaded = inputs[name]
        v.wait_ge(s[loaded], 16)
        v.quantize_mx(codes, scales, x).then_inc(s[name], 1)

    def fill(q):
        v.memset(T.qi[32:64, :], 0).then_inc(s.fill, 1)
        v.memset(T.qi[64:128, :], 0).then_inc(s.fill, 1)

    def mine(q):
        v.wait_ge(s.ldqp, 32)
        for i in range(4):
            v.tensor_copy(T.ql[32 * i:32 * i + 32, cols(OWN, 8)], T.qi[0:32, :]).then_inc(s.rep0, 1)
        v.wait_ge(s.rep0, 4)

    def out(q, o):
        q.wait_ge(s["y%d" % o], 1)
        dst, src = T.yb[:, cols(o)], bank(T, yb + o)
        (v.tensor_copy(dst, src) if q is v else a.activation(dst, src, COPY)).then_inc(s["yc%d" % o], 1)

    def adds(k, bs=range(4)):
        return [("add", b, k, 1) for b in bs]
    vector = [("fill",), ("pack", "qx"), ("mine",), ("wait", "ldkp", 16), ("keys",), ("offs", 0, OWN, 1), ("pack", "qr"), ("pack", "qk0"),
              ("pack", "qk1"), ("pack", "qv"), ("wait", "qpa", 16), ("repeat", 0, 2), ("offs", 0, 0, 2), ("pick", 0, 0, 1), ("pick", 2, 0, 1)]
    vector += adds(0) + [("relu", 0), ("quant", 0)] + adds(1) + [("quant", 1)]
    vector += adds(OWN) + [("relu", OWN), ("quant", OWN), ("out", 0)]
    scalar = [("copy", b) for b in range(4)] + [("pick", 1, 0, 1), ("pick", 3, 0, 1)] + [("pick", b, 1, 1) for b in range(4)]
    scalar += [("pick", 0, OWN, 1)] + [("relub", 1, b) for b in range(4)] + [("pick", b, OWN, 1) for b in range(1, 4)] + [("out", 1)]
    steps(g, T, first, vector, scalar, {"pack": pack, "fill": fill, "mine": mine, "out": out})

    for o, q in enumerate((g.sync, a)):
        q.wait_ge(s["yc%d" % o], 1)
        q.dma_start(T.y[:, cols(o)], T.yb[:, cols(o)]).then_inc(s.st, 16)
    g.sync.wait_ge(s.st, 32)
